import numpy as np
import ml_dtypes


def mxq(x, axis, fmt="e4m3"):
    dtype, down = {"e4m3": (ml_dtypes.float8_e4m3fn, 7), "e5m2": (ml_dtypes.float8_e5m2, 14)}[fmt]
    v = np.moveaxis(np.asarray(x, np.float32).astype(ml_dtypes.bfloat16).astype(np.float64), axis, -1)
    blocks = v.reshape(v.shape[:-1] + (-1, 32))
    amax = np.abs(blocks).max(-1, keepdims=True)
    byte = np.maximum(np.where(amax > 0, np.frexp(amax)[1] - 1 + 127, 0) - down, 1)
    scale = np.exp2(byte - 127.0)
    codes = (blocks / scale).astype(np.float32).astype(dtype).astype(np.float64)
    return np.moveaxis((codes * scale).reshape(v.shape), -1, axis)


WIDE = False


def mx_kscale(k):
    if not WIDE:
        return np.ones(k)
    levels = np.array([10, -10, 5, -5, 0])
    if k % 512:
        return np.exp2(np.random.permutation(np.resize(levels, k // 32))).repeat(32)
    a = np.empty((k // 512, 16))
    for p in range(k // 512):
        a[p, :8] = np.random.permutation(np.resize(levels, 8))
        for g in range(8):
            far = levels[np.abs(levels - a[p, g]) >= 10]
            a[p, g + 8] = far[np.random.randint(len(far))]
    return np.exp2(a.ravel()).repeat(32)


def f64(x):
    return np.asarray(x).astype(np.float64)


def striped(idx):
    return np.tile(idx.reshape(-1, 16).T, (8, 1)).astype(np.uint16)


def unstriped(offs):
    return offs[:16].T.reshape(-1).astype(np.int64)


E2M1 = np.array([0.0, 0.5, 1.0, 1.5, 2.0, 3.0, 4.0, 6.0, -0.0, -0.5, -1.0, -1.5, -2.0, -3.0, -4.0, -6.0])


def pack_weight(w, fmt):
    k, n = w.shape
    w = f64(np.asarray(w, np.float32).astype(ml_dtypes.bfloat16)).reshape(k // 32, 32, n)
    amax = np.abs(w).max(1)
    if fmt == "e4m3":
        byte = np.frexp(amax)[1] - 1 + 127 - 7
    else:
        mant, ex = np.frexp(amax / 6.0)
        byte = np.where(mant > 0.5, ex, ex - 1) + 127
    byte = np.clip(np.where(amax > 0, byte, 1), 1, 254)
    scaled = (w * np.exp2(127.0 - byte)[:, None, :]).reshape(k, n).astype(np.float32)
    by_word = np.ascontiguousarray(scaled.reshape(k // 512, 128, 4, n).transpose(0, 1, 3, 2))
    if fmt == "e4m3":
        words = by_word.astype(ml_dtypes.float8_e4m3fn).view(np.uint8)
    else:
        c = by_word.astype(ml_dtypes.float4_e2m1fn).view(np.uint8) & 0xF
        words = (c[..., 0::2] | (c[..., 1::2] << 4)).reshape(k // 512, 128, 2 * n)
    return np.ascontiguousarray(words), np.ascontiguousarray(byte.astype(np.uint8).reshape(k // 512, 16, n))


def unpack_weight(words, scales, fmt):
    g, _, n = scales.shape
    words = np.ascontiguousarray(words).reshape(g, 128, n, -1)
    if fmt == "e4m3":
        vals = words.view(ml_dtypes.float8_e4m3fn).astype(np.float64)
    else:
        nib = np.empty((g, 128, n, 4), np.uint8)
        nib[..., 0::2] = words & 0xF
        nib[..., 1::2] = words >> 4
        vals = E2M1[nib]
    vals = vals * np.repeat(np.exp2(scales.astype(np.float64) - 127.0), 8, axis=1)[..., None]
    return vals.transpose(0, 1, 3, 2).reshape(g * 512, n)


def pack_table(v):
    words, scales = pack_weight(v, "e4m3")
    return np.concatenate([words.reshape(words.shape[0], -1), scales.reshape(scales.shape[0], -1)], axis=1)


def unpack_table(tab):
    g, t = tab.shape[0], tab.shape[1] // 528
    return unpack_weight(tab[:, :512 * t].reshape(g, 128, t, 4), tab[:, 512 * t:].reshape(g, 16, t), "e4m3")


def gelu(v):
    return 0.5 * v * (1.0 + np.tanh(np.sqrt(2.0 / np.pi) * (v + 0.044715 * v**3)))


K, M, T, S = 2048, 1024, 1024, 512


def setup_inputs():
    n = np.random.standard_normal
    s = mx_kscale(K)[:, None]
    u = mx_kscale(512)[:, None]
    p_w4 = pack_weight(n((K, M)) / np.sqrt(K) / s, "e2m1")
    return {
        "tab": pack_table(n((K, T)) * s),
        "w4_words": p_w4[0],
        "w4_scales": p_w4[1],
        "down": (n((K, 512)) / np.sqrt(K) / s * u.T).astype(np.float32),
        "up": (0.5 * n((512, M)) / np.sqrt(512) / u).astype(np.float32),
        "b": (0.3 * n(1024)).astype(np.float32),
        "wgo": np.tile(np.random.uniform(0.5, 2.0, S), (128, 1)).astype(np.float32),
        "offs": striped(np.random.permutation(T)[:S]),
        "offs2": striped(np.random.permutation(T)[:S]),
    }


def reference(tab, w4_words, w4_scales, down, up, b, wgo, offs, offs2):
    tab_ = unpack_table(tab)[:, unstriped(offs)]
    w4_ = unpack_weight(w4_words, w4_scales, "e2m1")
    down_ = mxq(f64(down), 0, "e4m3")
    up_ = mxq(f64(up), 0, "e4m3")
    h_ = mxq(down_.T @ tab_, 0, "e4m3")
    y = w4_.T @ tab_ + up_.T @ h_
    out = np.zeros((M, T))
    out[:, unstriped(offs2)] = f64(wgo)[0] * (gelu(y + f64(b)[:, None]))
    return out

@@ -1,0 +1,294 @@
+from contextlib import ExitStack
+
+import concourse.mybir as mybir
+from concourse.masks import make_identity
+
+K, M, T, S, R = 2048, 1024, 1024, 512, 512
+FLOPS = 2 * S * (K * M + K * R + R * M)
+
+F32 = mybir.dt.float32
+BF16 = mybir.dt.bfloat16
+I32 = mybir.dt.int32
+U32 = mybir.dt.uint32
+U16 = mybir.dt.uint16
+U8 = mybir.dt.uint8
+FP8X4 = mybir.dt.float8_e4m3fn_x4
+FP4X4 = mybir.dt.float4_e2m1fn_x4
+GELU = mybir.ActivationFunctionType.Gelu_apprx_tanh
+MULT = mybir.AluOpType.mult
+
+P = 128
+PACK = 4
+K_PASS = P * PACK
+PASSES = K // K_PASS
+QUADS = 4
+CHUNK = 128
+CHUNKS = S // CHUNK
+TILES = M // P
+PAGES = 3
+UP_PIECES = ((0, 1), (1, 3), (3, 5), (5, 8))
+W4_PIECES = ((0, 2), (2, 4), (4, 8))
+W4_SCALE_PIECES = ((0, 2), (2, 8))
+
+
+def tile_list_tabscat_l_gelu_kernel(tc, tab, w4_words, w4_scales, down, up, b, wgo, offs, offs2, out):
+    nc = tc.nc
+    with ExitStack() as ctx:
+        keep = ctx.enter_context(tc.tile_pool(name="keep", bufs=1))
+        ring = ctx.enter_context(tc.tile_pool(name="ring", bufs=3))
+        psum = ctx.enter_context(tc.psum_pool(name="psum", bufs=4))
+
+        def held(shape, dtype, name, tag=None):
+            return keep.tile(shape, dtype, name=name, tag=tag or name, align_bytes=64)
+
+        pick = keep.tile([P, S // 16], U16, name="pick")
+        place = keep.tile([P, S // 16], U16, name="place")
+        tab_scales = held([P, T], U8, "tab_scales")
+        dense_scales = held([P, S], U8, "dense_scales")
+        got_scales = held([P, PASSES * S], U8, "got_scales")
+        tab_words = {}
+        got_words = [held([P, S], U32, f"got_words{a}") for a in range(PASSES)]
+        down_bf = [held([P, R * PACK], BF16, f"down_bf{a}") for a in range(PASSES)]
+        down_codes = [held([P, R], U32, f"down_codes{a}") for a in range(PASSES)]
+        down_scales = [held([P, R], U8, f"down_scales{a}") for a in range(PASSES)]
+        b_rows = held([P, P], F32, "b_rows")
+        identity = held([P, P], F32, "identity")
+        bias = held([P, TILES], F32, "bias")
+        warm = held([P, 16], F32, "warm")
+        pages = [held([P, T], F32, f"page{i}") for i in range(PAGES)]
+        w4_scale_tiles = {}
+
+        def clear_w4_scales(i, engine, tag=None):
+            lo, hi = W4_SCALE_PIECES[i]
+            w4_scale_tiles[i] = held([P, PASSES, (hi - lo) * P], U8, f"w4_scales{lo}", tag)
+            engine.memset(w4_scale_tiles[i][:].rearrange("p a n -> p (a n)").bitcast(I32), 0)
+
+        w4_tiles = {}
+        up_raw = {}
+        up_bf = {}
+        up_codes = held([P, M], U32, "up_codes")
+        up_scales = held([P, M], U8, "up_scales")
+        h_bf = [held([P, CHUNK * PACK], BF16, f"h_bf{c}") for c in range(CHUNKS)]
+        h_codes = held([P, S], U32, "h_codes")
+        h_scales = held([P, S], U8, "h_scales")
+
+        clear_w4_scales(0, nc.vector)
+        nc.vector.memset(b_rows[:], 0.0)
+        nc.vector.memset(tab_scales[64:128, :].bitcast(I32), 0)
+        nc.vector.memset(warm[:, 0:8], 0.0)
+        nc.scalar.activation(warm[:, 8:16], warm[:, 0:8], GELU)
+        nc.vector.memset(got_scales[:].bitcast(I32), 0)
+        for page in pages:
+            nc.vector.memset(page[:], 0.0)
+
+        def load_tab_words(a, tag=None):
+            tab_words[a] = held([P, T], I32, f"tab_words{a}", tag)
+            nc.sync.dma_start(tab_words[a][:], tab[a, 0 : K_PASS * T].bitcast(I32).rearrange("(p t) -> p t", p=P))
+
+        def load_down(a, lo, hi, tag=None):
+            raw = held([P, PACK, hi - lo], F32, f"down_raw{a}_{lo}", tag)
+            nc.sync.dma_start(raw[:], down[a * K_PASS : (a + 1) * K_PASS, lo:hi].rearrange("(p j) r -> p j r", j=PACK))
+            return raw
+
+        def load_up(i, tag=None):
+            lo, hi = UP_PIECES[i]
+            up_raw[i] = held([P, PACK, (hi - lo) * P], F32, f"up_raw{lo}", tag)
+            nc.sync.dma_start(up_raw[i][:], up[:, lo * P : hi * P].rearrange("(p j) n -> p j n", j=PACK))
+
+        def load_w4(i, tag=None):
+            lo, hi = W4_PIECES[i]
+            w4_tiles[i] = held([P, PASSES, (hi - lo) * P * 2], U8, f"w4_words{lo}", tag)
+            nc.sync.dma_start(w4_tiles[i][:].bitcast(I32), w4_words[:, :, 2 * lo * P : 2 * hi * P].bitcast(I32).rearrange("a p n -> p a n"))
+
+        def load_w4_scales(i, queue):
+            lo, hi = W4_SCALE_PIECES[i]
+            for q in range(QUADS):
+                queue.dma_start(
+                    w4_scale_tiles[i][32 * q : 32 * q + 4, :, :].bitcast(I32),
+                    w4_scales[:, 4 * q : 4 * q + 4, lo * P : hi * P].bitcast(I32).rearrange("a r n -> r a n"),
+                )
+
+        nc.sync.dma_start(pick[:], offs)
+        nc.sync.dma_start(
+            tab_scales[0:64, :].bitcast(I32),
+            tab[:, K_PASS * T :].bitcast(I32).rearrange("a (q t) -> q a t", q=16),
+        )
+        load_tab_words(0)
+        down_raw = [load_down(0, 0, R)]
+        load_tab_words(1)
+        down_raw.append(load_down(1, 0, R))
+        nc.sync.dma_start(place[:], offs2)
+        load_w4_scales(0, nc.sync)
+        nc.sync.dma_start(b_rows[0:TILES, :], b.rearrange("(c p) -> c p", p=P))
+
+        def gather(dst, window, lo, hi):
+            nc.vector.tensor_copy(dst[:, lo:hi], window.indirect(pick[:, lo // 16 : hi // 16]))
+
+        def cast_down(copy, a, raw, m_raw, m_lo, m_hi):
+            src = raw[:].rearrange("p j (m t) -> p m j t", t=PACK)[:, m_lo - m_raw : m_hi - m_raw]
+            dst = down_bf[a][:].rearrange("p (t m j) -> p m j t", t=PACK, j=PACK)[:, m_lo:m_hi]
+            copy(dst, src)
+
+        def quantize(codes, scales, values):
+            nc.vector.quantize_mx(out=codes.bitcast(FP8X4), scales=scales, in_=values)
+
+        def cast_up(copy, lo, hi, tag=None):
+            i, off = piece_of(UP_PIECES, lo)
+            up_bf[lo] = held([P, (hi - lo) * P * PACK], BF16, f"up_bf{lo}", tag)
+            copy(
+                up_bf[lo][:].rearrange("p (c i j) -> p c j i", i=4, j=PACK),
+                up_raw[i][:, :, off : off + (hi - lo) * P].rearrange("p j (c i) -> p c j i", i=4),
+            )
+
+        def quantize_up(lo, hi):
+            quantize(up_codes[:, lo * P : hi * P], up_scales[:, lo * P : hi * P], up_bf[lo][:])
+
+        h_banks = [psum.tile([P, PACK, CHUNK], F32, name=f"h_bank{c}", tag="h") for c in range(CHUNKS)]
+
+        def h_pass(a, c):
+            cols = slice(c * CHUNK, (c + 1) * CHUNK)
+            for t in range(PACK):
+                nc.tensor.matmul_mx(
+                    out=h_banks[c][:, t, :],
+                    lhsT=down_codes[a][:, t * P : (t + 1) * P].bitcast(FP8X4),
+                    lhsT_scale=down_scales[a][:, t * P : (t + 1) * P],
+                    rhs=got_words[a][:, cols].bitcast(FP8X4),
+                    rhs_scale=got_scales[:, a * S + cols.start : a * S + cols.stop],
+                    start=(a == 0 and t == 0),
+                    stop=(a == PASSES - 1 and t == PACK - 1),
+                )
+
+        def piece_of(pieces, n):
+            i = [lo <= n < hi for lo, hi in pieces].index(True)
+            return i, (n - pieces[i][0]) * P
+
+        def w4_passes(acc, n, cols):
+            wi, wo = piece_of(W4_PIECES, n)
+            si, so = piece_of(W4_SCALE_PIECES, n)
+            for a in range(PASSES):
+                nc.tensor.matmul_mx(
+                    out=acc,
+                    lhsT=w4_tiles[wi][:, a, 2 * wo : 2 * (wo + P)].bitcast(FP4X4),
+                    lhsT_scale=w4_scale_tiles[si][:, a, so : so + P],
+                    rhs=got_words[a][:, cols].bitcast(FP8X4),
+                    rhs_scale=got_scales[:, a * S + cols.start : a * S + cols.stop],
+                    start=(a == 0),
+                    stop=False,
+                )
+
+        def up_pass(acc, n, cols):
+            nc.tensor.matmul_mx(
+                out=acc,
+                lhsT=up_codes[:, n * P : (n + 1) * P].bitcast(FP8X4),
+                lhsT_scale=up_scales[:, n * P : (n + 1) * P],
+                rhs=h_codes[:, cols].bitcast(FP8X4),
+                rhs_scale=h_scales[:, cols],
+                start=False,
+                stop=True,
+            )
+
+        def gelu(acc, n, width, tag=None):
+            g = held([P, width], F32, tag) if tag else ring.tile([P, width], F32, name="g", tag="g")
+            nc.scalar.activation(g[:], acc, GELU, bias=bias[:, n : n + 1])
+            return g
+
+        def scatter(g, n, lo, hi):
+            nc.vector.tensor_tensor(pages[n % PAGES][:].indirect(place[:, lo // 16 : hi // 16]), g[:], weight[:, lo:hi], MULT)
+
+        def store(n):
+            nc.sync.dma_start(out[n * P : (n + 1) * P, :], pages[n % PAGES][:])
+
+        make_identity(nc, identity[:])
+        gather(dense_scales, tab_scales[:], 0, S)
+        for q in range(QUADS):
+            nc.sync.dma_start(
+                got_scales[32 * q : 32 * q + 4, :].bitcast(I32).rearrange("r (a s) -> r a s", a=PASSES),
+                dense_scales[16 * q : 16 * q + 16, :].bitcast(I32),
+            )
+        b_turned = psum.tile([P, P], F32, name="b_turned", tag="y")
+        nc.tensor.transpose(b_turned[:], b_rows[:], identity[:])
+        nc.scalar.copy(bias[:], b_turned[:, 0:TILES])
+
+        def gather_words(a, lo, hi):
+            gather(got_words[a], tab_words[a][:].bitcast(U32), lo, hi)
+
+        def cast_shared(a, raw, m_lo, m_hi, share=64):
+            cut = m_lo + share
+            cast_down(nc.vector.tensor_copy, a, raw, m_lo, m_lo, cut)
+            cast_down(nc.scalar.copy, a, raw, m_lo, cut, m_hi)
+
+        def finish_pass(a):
+            quantize(down_codes[a][:], down_scales[a][:], down_bf[a][:])
+            for c in range(CHUNKS):
+                h_pass(a, c)
+
+        gather_words(0, 0, S)
+        load_tab_words(2, "tab_words0")
+        cast_shared(0, down_raw[0], 0, P)
+        down_raw.append(load_down(2, 0, R, "down_raw0_0"))
+        finish_pass(0)
+        gather_words(1, 0, S)
+        first_half = load_down(3, 0, R // 2, "tab_words1")
+        cast_shared(1, down_raw[1], 0, P)
+        second_half = load_down(3, R // 2, R, "down_raw1_0")
+        finish_pass(1)
+        gather_words(2, 0, S)
+        load_tab_words(3, "tab_words0")
+        cast_shared(2, down_raw[2], 0, P)
+        load_up(0, "down_raw0_0")
+        finish_pass(2)
+        load_w4(0, "down_bf2")
+        last = PASSES - 1
+        cast_shared(last, first_half, 0, P // 2, 40)
+        weight = held([P, S], F32, "weight", "tab_words1")
+        nc.sync.dma_start(weight[:], wgo)
+        cast_shared(last, second_half, P // 2, P, 40)
+        load_up(1, "down_raw1_0")
+        quantize(down_codes[last][:], down_scales[last][:], down_bf[last][:])
+        clear_w4_scales(1, nc.gpsimd, "down_bf3")
+        load_w4_scales(1, nc.sync)
+        gather_words(last, 0, CHUNK)
+        h_pass(last, 0)
+        gather_words(last, CHUNK, S)
+        load_up(2, "tab_words0")
+        for c in range(1, CHUNKS):
+            h_pass(last, c)
+        cast_up(nc.vector.tensor_copy, 0, 1)
+        load_w4(1, "down_raw0_0")
+        quantize_up(0, 1)
+
+        for c in range(CHUNKS):
+            cols = slice(c * CHUNK, (c + 1) * CHUNK)
+            nc.scalar.copy(h_bf[c][:].rearrange("p (n t) -> p n t", t=PACK), h_banks[c][:].rearrange("p t n -> p n t"))
+            quantize(h_codes[:, cols], h_scales[:, cols], h_bf[c][:])
+            if c == 0:
+                load_up(3, "up_bf0")
+                load_w4(2, "h_bf0")
+            acc = psum.tile([P, CHUNK], F32, name="acc", tag="y")
+            w4_passes(acc[:], 0, cols)
+            up_pass(acc[:], 0, cols)
+            scatter(gelu(acc[:], 0, CHUNK, f"g_chunk{c}"), 0, c * CHUNK, (c + 1) * CHUNK)
+        store(0)
+
+        def whole_tile(n, tag=None):
+            acc = psum.tile([P, S], F32, name="acc", tag="y")
+            w4_passes(acc[:], n, slice(0, S))
+            up_pass(acc[:], n, slice(0, S))
+            scatter(gelu(acc[:], n, S, tag), n, 0, S)
+            store(n)
+
+        cast_up(nc.scalar.copy, 1, 2, "h_bf1")
+        cast_up(nc.scalar.copy, 2, 3, "h_bf2")
+        quantize_up(1, 2)
+        quantize_up(2, 3)
+        whole_tile(1, "g_tile1")
+        cast_up(nc.scalar.copy, 3, 5, "g_chunk3")
+        quantize_up(3, 5)
+        whole_tile(2)
+        whole_tile(3)
+        cast_up(nc.scalar.copy, 5, 7, "g_tile1")
+        cast_up(nc.scalar.copy, 7, 8)
+        quantize_up(5, 7)
+        quantize_up(7, 8)
+        for n in range(4, TILES):
+            whole_tile(n)

@@ -53,7 +53,6 @@ def tile_list_tabscat_l_gelu_kernel(tc, tab, w4_words, w4_scales, down, up, b, w
         down_scales = [held([P, R], U8, f"down_scales{a}") for a in range(PASSES)]
         b_rows = held([P, P], F32, "b_rows")
         identity = held([P, P], F32, "identity")
-        bias = held([P, TILES], F32, "bias")
         warm = held([P, 16], F32, "warm")
         pages = [held([P, T], F32, f"page{i}") for i in range(PAGES)]
         w4_scale_tiles = {}
@@ -72,14 +71,12 @@ def tile_list_tabscat_l_gelu_kernel(tc, tab, w4_words, w4_scales, down, up, b, w
         h_codes = held([P, S], U32, "h_codes")
         h_scales = held([P, S], U8, "h_scales")
 
-        clear_w4_scales(0, nc.vector)
         nc.vector.memset(b_rows[:], 0.0)
+        clear_w4_scales(0, nc.vector)
         nc.vector.memset(tab_scales[64:128, :].bitcast(I32), 0)
         nc.vector.memset(warm[:, 0:8], 0.0)
         nc.scalar.activation(warm[:, 8:16], warm[:, 0:8], GELU)
         nc.vector.memset(got_scales[:].bitcast(I32), 0)
-        for page in pages:
-            nc.vector.memset(page[:], 0.0)
 
         def load_tab_words(a, tag=None):
             tab_words[a] = held([P, T], I32, f"tab_words{a}", tag)
@@ -102,10 +99,10 @@ def tile_list_tabscat_l_gelu_kernel(tc, tab, w4_words, w4_scales, down, up, b, w
 
         def load_w4_scales(i, queue):
             lo, hi = W4_SCALE_PIECES[i]
-            for q in range(QUADS):
+            for r in range(4):
                 queue.dma_start(
-                    w4_scale_tiles[i][32 * q : 32 * q + 4, :, :].bitcast(I32),
-                    w4_scales[:, 4 * q : 4 * q + 4, lo * P : hi * P].bitcast(I32).rearrange("a r n -> r a n"),
+                    w4_scale_tiles[i][r:P:32, :, :].bitcast(I32),
+                    w4_scales[:, r:16:4, lo * P : hi * P].bitcast(I32).rearrange("a q n -> q a n"),
                 )
 
         nc.sync.dma_start(pick[:], offs)
@@ -118,8 +115,8 @@ def tile_list_tabscat_l_gelu_kernel(tc, tab, w4_words, w4_scales, down, up, b, w
         load_tab_words(1)
         down_raw.append(load_down(1, 0, R))
         nc.sync.dma_start(place[:], offs2)
-        load_w4_scales(0, nc.sync)
-        nc.sync.dma_start(b_rows[0:TILES, :], b.rearrange("(c p) -> c p", p=P))
+        nc.gpsimd.dma_start(b_rows[0:TILES, :], b.rearrange("(c p) -> c p", p=P))
+        load_w4_scales(0, nc.gpsimd)
 
         def gather(dst, window, lo, hi):
             nc.vector.tensor_copy(dst[:, lo:hi], window.indirect(pick[:, lo // 16 : hi // 16]))
@@ -199,14 +196,18 @@ def tile_list_tabscat_l_gelu_kernel(tc, tab, w4_words, w4_scales, down, up, b, w
             nc.sync.dma_start(out[n * P : (n + 1) * P, :], pages[n % PAGES][:])
 
         make_identity(nc, identity[:])
+        for page in pages:
+            nc.gpsimd.memset(page[:], 0.0)
         gather(dense_scales, tab_scales[:], 0, S)
         for q in range(QUADS):
             nc.sync.dma_start(
                 got_scales[32 * q : 32 * q + 4, :].bitcast(I32).rearrange("r (a s) -> r a s", a=PASSES),
                 dense_scales[16 * q : 16 * q + 16, :].bitcast(I32),
             )
+        load_tab_words(2, "tab_scales")
         b_turned = psum.tile([P, P], F32, name="b_turned", tag="y")
         nc.tensor.transpose(b_turned[:], b_rows[:], identity[:])
+        bias = held([P, TILES], F32, "bias", "dense_scales")
         nc.scalar.copy(bias[:], b_turned[:, 0:TILES])
 
         def gather_words(a, lo, hi):
@@ -223,47 +224,45 @@ def tile_list_tabscat_l_gelu_kernel(tc, tab, w4_words, w4_scales, down, up, b, w
                 h_pass(a, c)
 
         gather_words(0, 0, S)
-        load_tab_words(2, "tab_words0")
+        down_raw.append(load_down(2, 0, R, "tab_words0"))
         cast_shared(0, down_raw[0], 0, P)
-        down_raw.append(load_down(2, 0, R, "down_raw0_0"))
+        first_half = load_down(3, 0, R // 2, "down_raw0_0")
         finish_pass(0)
+        second_half = load_down(3, R // 2, R, "down_bf0")
         gather_words(1, 0, S)
-        first_half = load_down(3, 0, R // 2, "tab_words1")
+        load_tab_words(3, "tab_words1")
         cast_shared(1, down_raw[1], 0, P)
-        second_half = load_down(3, R // 2, R, "down_raw1_0")
+        load_up(0, "down_raw1_0")
         finish_pass(1)
+        load_w4(0, "down_bf1")
         gather_words(2, 0, S)
-        load_tab_words(3, "tab_words0")
+        weight = held([P, S], F32, "weight", "tab_scales")
+        nc.sync.dma_start(weight[:], wgo)
         cast_shared(2, down_raw[2], 0, P)
-        load_up(0, "down_raw0_0")
+        load_up(1, "tab_words0")
         finish_pass(2)
-        load_w4(0, "down_bf2")
         last = PASSES - 1
         cast_shared(last, first_half, 0, P // 2, 40)
-        weight = held([P, S], F32, "weight", "tab_words1")
-        nc.sync.dma_start(weight[:], wgo)
+        load_w4(1, "down_raw0_0")
+        load_up(2, "down_bf2")
         cast_shared(last, second_half, P // 2, P, 40)
-        load_up(1, "down_raw1_0")
         quantize(down_codes[last][:], down_scales[last][:], down_bf[last][:])
         clear_w4_scales(1, nc.gpsimd, "down_bf3")
         load_w4_scales(1, nc.sync)
         gather_words(last, 0, CHUNK)
         h_pass(last, 0)
         gather_words(last, CHUNK, S)
-        load_up(2, "tab_words0")
+        load_up(3, "tab_words1")
         for c in range(1, CHUNKS):
             h_pass(last, c)
         cast_up(nc.vector.tensor_copy, 0, 1)
-        load_w4(1, "down_raw0_0")
+        load_w4(2, "down_raw1_0")
         quantize_up(0, 1)
 
         for c in range(CHUNKS):
             cols = slice(c * CHUNK, (c + 1) * CHUNK)
             nc.scalar.copy(h_bf[c][:].rearrange("p (n t) -> p n t", t=PACK), h_banks[c][:].rearrange("p t n -> p n t"))
             quantize(h_codes[:, cols], h_scales[:, cols], h_bf[c][:])
-            if c == 0:
-                load_up(3, "up_bf0")
-                load_w4(2, "h_bf0")
             acc = psum.tile([P, CHUNK], F32, name="acc", tag="y")
             w4_passes(acc[:], 0, cols)
             up_pass(acc[:], 0, cols)

@@ -21,33 +21,51 @@ P = 128
 PACK = 4
 K_PASS = P * PACK
 PASSES = K // K_PASS
-QUADS = 4
+LAST = PASSES - 1
+BLOCKS = K_PASS // 32
+QUAD = 32
+QUAD_ROWS = 4
+ENTRIES = 16
+LINE = 4
 CHUNK = 128
 CHUNKS = S // CHUNK
 TILES = M // P
 PAGES = 3
+GELU_BUFS = 3
+PSUM_BUFS = 4
+
 UP_PIECES = ((0, 1), (1, 3), (3, 5), (5, 8))
 W4_PIECES = ((0, 2), (2, 4), (4, 8))
 W4_SCALE_PIECES = ((0, 2), (2, 8))
+
+SHARE_WHOLE = 64
+SHARE_HALF = 40
+
+
+def piece_of(pieces, n):
+    i = [lo <= n < hi for lo, hi in pieces].index(True)
+    return i, (n - pieces[i][0]) * P
 
 
 def tile_list_tabscat_l_gelu_kernel(tc, tab, w4_words, w4_scales, down, up, b, wgo, offs, offs2, out):
     nc = tc.nc
     with ExitStack() as ctx:
         keep = ctx.enter_context(tc.tile_pool(name="keep", bufs=1))
-        ring = ctx.enter_context(tc.tile_pool(name="ring", bufs=3))
-        psum = ctx.enter_context(tc.psum_pool(name="psum", bufs=4))
+        ring = ctx.enter_context(tc.tile_pool(name="ring", bufs=GELU_BUFS))
+        psum = ctx.enter_context(tc.psum_pool(name="psum", bufs=PSUM_BUFS))
 
-        def held(shape, dtype, name, tag=None):
-            return keep.tile(shape, dtype, name=name, tag=tag or name, align_bytes=64)
+        def held(shape, dtype, name, reuse=None):
+            return keep.tile(shape, dtype, name=name, tag=reuse or name, align_bytes=64)
 
-        pick = keep.tile([P, S // 16], U16, name="pick")
-        place = keep.tile([P, S // 16], U16, name="place")
+        pick = keep.tile([P, S // ENTRIES], U16, name="pick")
+        place = keep.tile([P, S // ENTRIES], U16, name="place")
         tab_scales = held([P, T], U8, "tab_scales")
         dense_scales = held([P, S], U8, "dense_scales")
         got_scales = held([P, PASSES * S], U8, "got_scales")
         tab_words = {}
-        got_words = [held([P, S], U32, f"got_words{a}") for a in range(PASSES)]
+        got_words = [held([P, S], U32, f"got_words{a}") for a in range(LAST)]
+        got_words.append(held([P, S - CHUNK], U32, f"got_words{LAST}"))
+        got_tail = []
         down_bf = [held([P, R * PACK], BF16, f"down_bf{a}") for a in range(PASSES)]
         down_codes = [held([P, R], U32, f"down_codes{a}") for a in range(PASSES)]
         down_scales = [held([P, R], U8, f"down_scales{a}") for a in range(PASSES)]
@@ -56,12 +74,6 @@ def tile_list_tabscat_l_gelu_kernel(tc, tab, w4_words, w4_scales, down, up, b, w
         warm = held([P, 16], F32, "warm")
         pages = [held([P, T], F32, f"page{i}") for i in range(PAGES)]
         w4_scale_tiles = {}
-
-        def clear_w4_scales(i, engine, tag=None):
-            lo, hi = W4_SCALE_PIECES[i]
-            w4_scale_tiles[i] = held([P, PASSES, (hi - lo) * P], U8, f"w4_scales{lo}", tag)
-            engine.memset(w4_scale_tiles[i][:].rearrange("p a n -> p (a n)").bitcast(I32), 0)
-
         w4_tiles = {}
         up_raw = {}
         up_bf = {}
@@ -70,45 +82,150 @@ def tile_list_tabscat_l_gelu_kernel(tc, tab, w4_words, w4_scales, down, up, b, w
         h_bf = [held([P, CHUNK * PACK], BF16, f"h_bf{c}") for c in range(CHUNKS)]
         h_codes = held([P, S], U32, "h_codes")
         h_scales = held([P, S], U8, "h_scales")
+        h_banks = [psum.tile([P, PACK, CHUNK], F32, name=f"h_bank{c}", tag="h") for c in range(CHUNKS)]
+
+
+        def load_tab_words(a, reuse=None):
+            tab_words[a] = held([P, T], I32, f"tab_words{a}", reuse)
+            nc.sync.dma_start(tab_words[a][:], tab[a, 0 : K_PASS * T].bitcast(I32).rearrange("(p t) -> p t", p=P))
+
+        def load_down(a, lo, hi, reuse=None):
+            raw = held([P, PACK, hi - lo], F32, f"down_raw{a}_{lo}", reuse)
+            nc.sync.dma_start(raw[:], down[a * K_PASS : (a + 1) * K_PASS, lo:hi].rearrange("(p j) r -> p j r", j=PACK))
+            return raw
+
+        def load_up(i, reuse):
+            lo, hi = UP_PIECES[i]
+            up_raw[i] = held([P, PACK, (hi - lo) * P], F32, f"up_raw{lo}", reuse)
+            nc.sync.dma_start(up_raw[i][:], up[:, lo * P : hi * P].rearrange("(p j) n -> p j n", j=PACK))
+
+        def load_w4(i, reuse):
+            lo, hi = W4_PIECES[i]
+            w4_tiles[i] = held([P, PASSES, (hi - lo) * P * 2], U8, f"w4_words{lo}", reuse)
+            nc.sync.dma_start(
+                w4_tiles[i][:].bitcast(I32),
+                w4_words[:, :, 2 * lo * P : 2 * hi * P].bitcast(I32).rearrange("a p n -> p a n"),
+            )
+
+        def clear_w4_scales(i, engine, reuse=None):
+            lo, hi = W4_SCALE_PIECES[i]
+            w4_scale_tiles[i] = held([P, PASSES, (hi - lo) * P], U8, f"w4_scales{lo}", reuse)
+            engine.memset(w4_scale_tiles[i][:].rearrange("p a n -> p (a n)").bitcast(I32), 0)
+
+        def load_w4_scales(i, queue):
+            lo, hi = W4_SCALE_PIECES[i]
+            for r in range(QUAD_ROWS):
+                queue.dma_start(
+                    w4_scale_tiles[i][r:P:QUAD, :, :].bitcast(I32),
+                    w4_scales[:, r:BLOCKS:QUAD_ROWS, lo * P : hi * P].bitcast(I32).rearrange("a q n -> q a n"),
+                )
+
+
+        def gather(dst, window, lo, hi):
+            nc.vector.tensor_copy(dst, window.indirect(pick[:, lo // ENTRIES : hi // ENTRIES]))
+
+        def gather_words(a, lo, hi):
+            gather(got_words[a][:, lo:hi], tab_words[a][:].bitcast(U32), lo, hi)
+
+        def cast_down(a, raw, m_lo, m_hi, share):
+            src = raw[:].rearrange("p j (m t) -> p m j t", t=PACK)
+            dst = down_bf[a][:].rearrange("p (t m j) -> p m j t", t=PACK, j=PACK)
+            nc.vector.tensor_copy(dst[:, m_lo : m_lo + share], src[:, 0:share])
+            nc.scalar.copy(dst[:, m_lo + share : m_hi], src[:, share : m_hi - m_lo])
+
+        def cast_up(copy, lo, hi, reuse=None):
+            i, first = piece_of(UP_PIECES, lo)
+            up_bf[lo] = held([P, (hi - lo) * P * PACK], BF16, f"up_bf{lo}", reuse)
+            copy(
+                up_bf[lo][:].rearrange("p (c i j) -> p c j i", i=LINE, j=PACK),
+                up_raw[i][:, :, first : first + (hi - lo) * P].rearrange("p j (c i) -> p c j i", i=LINE),
+            )
+
+        def quantize(codes, scales, values):
+            nc.vector.quantize_mx(out=codes.bitcast(FP8X4), scales=scales, in_=values)
+
+        def quantize_down(a):
+            quantize(down_codes[a][:], down_scales[a][:], down_bf[a][:])
+
+        def quantize_up(lo, hi):
+            quantize(up_codes[:, lo * P : hi * P], up_scales[:, lo * P : hi * P], up_bf[lo][:])
+
+        def quantize_h(c):
+            cols = chunk_cols(c)
+            nc.scalar.copy(h_bf[c][:].rearrange("p (n t) -> p n t", t=PACK), h_banks[c][:].rearrange("p t n -> p n t"))
+            quantize(h_codes[:, cols], h_scales[:, cols], h_bf[c][:])
+
+        def gelu(g, acc, n):
+            nc.scalar.activation(g, acc[:], GELU, bias=bias[:, n : n + 1])
+
+        def scatter(g, n, lo, hi):
+            window = pages[n % PAGES][:].indirect(place[:, lo // ENTRIES : hi // ENTRIES])
+            nc.vector.tensor_tensor(window, g[:], weight[:, lo:hi], MULT)
+
+        def store(n):
+            nc.sync.dma_start(out[n * P : (n + 1) * P, :], pages[n % PAGES][:])
+
+
+        def chunk_cols(c):
+            return slice(c * CHUNK, (c + 1) * CHUNK)
+
+        def words_of(a, cols):
+            if a == LAST and cols.start == S - CHUNK:
+                return got_tail[0][:]
+            return got_words[a][:, cols]
+
+        def h_pass(a, c):
+            cols = chunk_cols(c)
+            for t in range(PACK):
+                nc.tensor.matmul_mx(
+                    out=h_banks[c][:, t, :],
+                    lhsT=down_codes[a][:, t * P : (t + 1) * P].bitcast(FP8X4),
+                    lhsT_scale=down_scales[a][:, t * P : (t + 1) * P],
+                    rhs=words_of(a, cols).bitcast(FP8X4),
+                    rhs_scale=got_scales[:, a * S + cols.start : a * S + cols.stop],
+                    start=(a == 0 and t == 0),
+                    stop=(a == LAST and t == PACK - 1),
+                )
+
+        def y_sum(n, cols):
+            acc = psum.tile([P, cols.stop - cols.start], F32, name="acc", tag="y")
+            wi, w_first = piece_of(W4_PIECES, n)
+            si, s_first = piece_of(W4_SCALE_PIECES, n)
+            for a in range(PASSES):
+                width = CHUNK if a == LAST else cols.stop - cols.start
+                for lo in range(cols.start, cols.stop, width):
+                    nc.tensor.matmul_mx(
+                        out=acc[:, lo - cols.start : lo - cols.start + width],
+                        lhsT=w4_tiles[wi][:, a, 2 * w_first : 2 * (w_first + P)].bitcast(FP4X4),
+                        lhsT_scale=w4_scale_tiles[si][:, a, s_first : s_first + P],
+                        rhs=words_of(a, slice(lo, lo + width)).bitcast(FP8X4),
+                        rhs_scale=got_scales[:, a * S + lo : a * S + lo + width],
+                        start=(a == 0),
+                        stop=False,
+                    )
+            nc.tensor.matmul_mx(
+                out=acc[:],
+                lhsT=up_codes[:, n * P : (n + 1) * P].bitcast(FP8X4),
+                lhsT_scale=up_scales[:, n * P : (n + 1) * P],
+                rhs=h_codes[:, cols].bitcast(FP8X4),
+                rhs_scale=h_scales[:, cols],
+                start=False,
+                stop=True,
+            )
+            return acc
+
 
         nc.vector.memset(b_rows[:], 0.0)
         clear_w4_scales(0, nc.vector)
-        nc.vector.memset(tab_scales[64:128, :].bitcast(I32), 0)
+        nc.vector.memset(tab_scales[PASSES * BLOCKS : P, :].bitcast(I32), 0)
         nc.vector.memset(warm[:, 0:8], 0.0)
         nc.scalar.activation(warm[:, 8:16], warm[:, 0:8], GELU)
         nc.vector.memset(got_scales[:].bitcast(I32), 0)
 
-        def load_tab_words(a, tag=None):
-            tab_words[a] = held([P, T], I32, f"tab_words{a}", tag)
-            nc.sync.dma_start(tab_words[a][:], tab[a, 0 : K_PASS * T].bitcast(I32).rearrange("(p t) -> p t", p=P))
-
-        def load_down(a, lo, hi, tag=None):
-            raw = held([P, PACK, hi - lo], F32, f"down_raw{a}_{lo}", tag)
-            nc.sync.dma_start(raw[:], down[a * K_PASS : (a + 1) * K_PASS, lo:hi].rearrange("(p j) r -> p j r", j=PACK))
-            return raw
-
-        def load_up(i, tag=None):
-            lo, hi = UP_PIECES[i]
-            up_raw[i] = held([P, PACK, (hi - lo) * P], F32, f"up_raw{lo}", tag)
-            nc.sync.dma_start(up_raw[i][:], up[:, lo * P : hi * P].rearrange("(p j) n -> p j n", j=PACK))
-
-        def load_w4(i, tag=None):
-            lo, hi = W4_PIECES[i]
-            w4_tiles[i] = held([P, PASSES, (hi - lo) * P * 2], U8, f"w4_words{lo}", tag)
-            nc.sync.dma_start(w4_tiles[i][:].bitcast(I32), w4_words[:, :, 2 * lo * P : 2 * hi * P].bitcast(I32).rearrange("a p n -> p a n"))
-
-        def load_w4_scales(i, queue):
-            lo, hi = W4_SCALE_PIECES[i]
-            for r in range(4):
-                queue.dma_start(
-                    w4_scale_tiles[i][r:P:32, :, :].bitcast(I32),
-                    w4_scales[:, r:16:4, lo * P : hi * P].bitcast(I32).rearrange("a q n -> q a n"),
-                )
-
         nc.sync.dma_start(pick[:], offs)
         nc.sync.dma_start(
-            tab_scales[0:64, :].bitcast(I32),
-            tab[:, K_PASS * T :].bitcast(I32).rearrange("a (q t) -> q a t", q=16),
+            tab_scales[0 : PASSES * BLOCKS, :].bitcast(I32),
+            tab[:, K_PASS * T :].bitcast(I32).rearrange("a (q t) -> q a t", q=BLOCKS),
         )
         load_tab_words(0)
         down_raw = [load_down(0, 0, R)]
@@ -117,177 +234,115 @@ def tile_list_tabscat_l_gelu_kernel(tc, tab, w4_words, w4_scales, down, up, b, w
         nc.sync.dma_start(place[:], offs2)
         nc.gpsimd.dma_start(b_rows[0:TILES, :], b.rearrange("(c p) -> c p", p=P))
         load_w4_scales(0, nc.gpsimd)
-
-        def gather(dst, window, lo, hi):
-            nc.vector.tensor_copy(dst[:, lo:hi], window.indirect(pick[:, lo // 16 : hi // 16]))
-
-        def cast_down(copy, a, raw, m_raw, m_lo, m_hi):
-            src = raw[:].rearrange("p j (m t) -> p m j t", t=PACK)[:, m_lo - m_raw : m_hi - m_raw]
-            dst = down_bf[a][:].rearrange("p (t m j) -> p m j t", t=PACK, j=PACK)[:, m_lo:m_hi]
-            copy(dst, src)
-
-        def quantize(codes, scales, values):
-            nc.vector.quantize_mx(out=codes.bitcast(FP8X4), scales=scales, in_=values)
-
-        def cast_up(copy, lo, hi, tag=None):
-            i, off = piece_of(UP_PIECES, lo)
-            up_bf[lo] = held([P, (hi - lo) * P * PACK], BF16, f"up_bf{lo}", tag)
-            copy(
-                up_bf[lo][:].rearrange("p (c i j) -> p c j i", i=4, j=PACK),
-                up_raw[i][:, :, off : off + (hi - lo) * P].rearrange("p j (c i) -> p c j i", i=4),
-            )
-
-        def quantize_up(lo, hi):
-            quantize(up_codes[:, lo * P : hi * P], up_scales[:, lo * P : hi * P], up_bf[lo][:])
-
-        h_banks = [psum.tile([P, PACK, CHUNK], F32, name=f"h_bank{c}", tag="h") for c in range(CHUNKS)]
-
-        def h_pass(a, c):
-            cols = slice(c * CHUNK, (c + 1) * CHUNK)
-            for t in range(PACK):
-                nc.tensor.matmul_mx(
-                    out=h_banks[c][:, t, :],
-                    lhsT=down_codes[a][:, t * P : (t + 1) * P].bitcast(FP8X4),
-                    lhsT_scale=down_scales[a][:, t * P : (t + 1) * P],
-                    rhs=got_words[a][:, cols].bitcast(FP8X4),
-                    rhs_scale=got_scales[:, a * S + cols.start : a * S + cols.stop],
-                    start=(a == 0 and t == 0),
-                    stop=(a == PASSES - 1 and t == PACK - 1),
-                )
-
-        def piece_of(pieces, n):
-            i = [lo <= n < hi for lo, hi in pieces].index(True)
-            return i, (n - pieces[i][0]) * P
-
-        def w4_passes(acc, n, cols):
-            wi, wo = piece_of(W4_PIECES, n)
-            si, so = piece_of(W4_SCALE_PIECES, n)
-            for a in range(PASSES):
-                nc.tensor.matmul_mx(
-                    out=acc,
-                    lhsT=w4_tiles[wi][:, a, 2 * wo : 2 * (wo + P)].bitcast(FP4X4),
-                    lhsT_scale=w4_scale_tiles[si][:, a, so : so + P],
-                    rhs=got_words[a][:, cols].bitcast(FP8X4),
-                    rhs_scale=got_scales[:, a * S + cols.start : a * S + cols.stop],
-                    start=(a == 0),
-                    stop=False,
-                )
-
-        def up_pass(acc, n, cols):
-            nc.tensor.matmul_mx(
-                out=acc,
-                lhsT=up_codes[:, n * P : (n + 1) * P].bitcast(FP8X4),
-                lhsT_scale=up_scales[:, n * P : (n + 1) * P],
-                rhs=h_codes[:, cols].bitcast(FP8X4),
-                rhs_scale=h_scales[:, cols],
-                start=False,
-                stop=True,
-            )
-
-        def gelu(acc, n, width, tag=None):
-            g = held([P, width], F32, tag) if tag else ring.tile([P, width], F32, name="g", tag="g")
-            nc.scalar.activation(g[:], acc, GELU, bias=bias[:, n : n + 1])
-            return g
-
-        def scatter(g, n, lo, hi):
-            nc.vector.tensor_tensor(pages[n % PAGES][:].indirect(place[:, lo // 16 : hi // 16]), g[:], weight[:, lo:hi], MULT)
-
-        def store(n):
-            nc.sync.dma_start(out[n * P : (n + 1) * P, :], pages[n % PAGES][:])
-
         make_identity(nc, identity[:])
         for page in pages:
             nc.gpsimd.memset(page[:], 0.0)
-        gather(dense_scales, tab_scales[:], 0, S)
-        for q in range(QUADS):
+
+
+        gather(dense_scales[:], tab_scales[:], 0, S)
+        dense_rows = QUAD_ROWS * PASSES
+        for q in range(P // QUAD):
             nc.sync.dma_start(
-                got_scales[32 * q : 32 * q + 4, :].bitcast(I32).rearrange("r (a s) -> r a s", a=PASSES),
-                dense_scales[16 * q : 16 * q + 16, :].bitcast(I32),
+                got_scales[QUAD * q : QUAD * q + QUAD_ROWS, :].bitcast(I32).rearrange("r (a s) -> r a s", a=PASSES),
+                dense_scales[dense_rows * q : dense_rows * (q + 1), :].bitcast(I32),
             )
-        load_tab_words(2, "tab_scales")
+        down_raw.append(load_down(2, 0, R, reuse="tab_scales"))
+
         b_turned = psum.tile([P, P], F32, name="b_turned", tag="y")
         nc.tensor.transpose(b_turned[:], b_rows[:], identity[:])
-        bias = held([P, TILES], F32, "bias", "dense_scales")
+        bias = held([P, TILES], F32, "bias", reuse="dense_scales")
         nc.scalar.copy(bias[:], b_turned[:, 0:TILES])
 
-        def gather_words(a, lo, hi):
-            gather(got_words[a], tab_words[a][:].bitcast(U32), lo, hi)
-
-        def cast_shared(a, raw, m_lo, m_hi, share=64):
-            cut = m_lo + share
-            cast_down(nc.vector.tensor_copy, a, raw, m_lo, m_lo, cut)
-            cast_down(nc.scalar.copy, a, raw, m_lo, cut, m_hi)
-
-        def finish_pass(a):
-            quantize(down_codes[a][:], down_scales[a][:], down_bf[a][:])
-            for c in range(CHUNKS):
-                h_pass(a, c)
 
         gather_words(0, 0, S)
-        down_raw.append(load_down(2, 0, R, "tab_words0"))
-        cast_shared(0, down_raw[0], 0, P)
-        first_half = load_down(3, 0, R // 2, "down_raw0_0")
-        finish_pass(0)
-        second_half = load_down(3, R // 2, R, "down_bf0")
-        gather_words(1, 0, S)
-        load_tab_words(3, "tab_words1")
-        cast_shared(1, down_raw[1], 0, P)
-        load_up(0, "down_raw1_0")
-        finish_pass(1)
-        load_w4(0, "down_bf1")
-        gather_words(2, 0, S)
-        weight = held([P, S], F32, "weight", "tab_scales")
-        nc.sync.dma_start(weight[:], wgo)
-        cast_shared(2, down_raw[2], 0, P)
-        load_up(1, "tab_words0")
-        finish_pass(2)
-        last = PASSES - 1
-        cast_shared(last, first_half, 0, P // 2, 40)
-        load_w4(1, "down_raw0_0")
-        load_up(2, "down_bf2")
-        cast_shared(last, second_half, P // 2, P, 40)
-        quantize(down_codes[last][:], down_scales[last][:], down_bf[last][:])
-        clear_w4_scales(1, nc.gpsimd, "down_bf3")
-        load_w4_scales(1, nc.sync)
-        gather_words(last, 0, CHUNK)
-        h_pass(last, 0)
-        gather_words(last, CHUNK, S)
-        load_up(3, "tab_words1")
-        for c in range(1, CHUNKS):
-            h_pass(last, c)
-        cast_up(nc.vector.tensor_copy, 0, 1)
-        load_w4(2, "down_raw1_0")
-        quantize_up(0, 1)
-
+        load_tab_words(2, reuse="tab_words0")
+        cast_down(0, down_raw[0], 0, P, SHARE_WHOLE)
+        first_half = load_down(LAST, 0, R // 2, reuse="down_raw0_0")
+        quantize_down(0)
         for c in range(CHUNKS):
-            cols = slice(c * CHUNK, (c + 1) * CHUNK)
-            nc.scalar.copy(h_bf[c][:].rearrange("p (n t) -> p n t", t=PACK), h_banks[c][:].rearrange("p t n -> p n t"))
-            quantize(h_codes[:, cols], h_scales[:, cols], h_bf[c][:])
-            acc = psum.tile([P, CHUNK], F32, name="acc", tag="y")
-            w4_passes(acc[:], 0, cols)
-            up_pass(acc[:], 0, cols)
-            scatter(gelu(acc[:], 0, CHUNK, f"g_chunk{c}"), 0, c * CHUNK, (c + 1) * CHUNK)
+            h_pass(0, c)
+        second_half = load_down(LAST, R // 2, R, reuse="down_bf0")
+
+        gather_words(1, 0, S)
+        load_tab_words(LAST, reuse="tab_words1")
+        cast_down(1, down_raw[1], 0, P, SHARE_WHOLE)
+        load_up(0, reuse="down_raw1_0")
+        quantize_down(1)
+        for c in range(CHUNKS):
+            h_pass(1, c)
+        load_w4(0, reuse="down_bf1")
+
+        cast_down(2, down_raw[2], 0, P, SHARE_WHOLE)
+        weight = held([P, S], F32, "weight", reuse="tab_scales")
+        nc.sync.dma_start(weight[:], wgo)
+        quantize_down(2)
+        for half in range(2):
+            gather_words(2, half * S // 2, (half + 1) * S // 2)
+            for c in range(half * CHUNKS // 2, (half + 1) * CHUNKS // 2):
+                h_pass(2, c)
+        load_up(1, reuse="tab_words0")
+
+        cast_down(LAST, first_half, 0, P // 2, SHARE_HALF)
+        load_w4(1, reuse="down_raw0_0")
+        cast_down(LAST, second_half, P // 2, P, SHARE_HALF)
+        load_up(2, reuse="down_bf0")
+        quantize_down(LAST)
+        clear_w4_scales(1, nc.gpsimd, reuse=f"down_bf{LAST}")
+        load_w4_scales(1, nc.sync)
+        gather_words(LAST, 0, CHUNK)
+        h_pass(LAST, 0)
+        gather_words(LAST, CHUNK, S - CHUNK)
+        for c in range(1, CHUNKS - 1):
+            h_pass(LAST, c)
+        cast_up(nc.vector.tensor_copy, 0, 1)
+        load_w4(2, reuse="down_raw1_0")
+
+
+        quantize_h(0)
+        quantize_up(0, 1)
+        got_tail.append(held([P, CHUNK], U32, "got_tail", reuse="h_bf0"))
+        gather(got_tail[0][:], tab_words[LAST][:].bitcast(U32), S - CHUNK, S)
+        load_up(3, reuse="tab_words1")
+        acc = y_sum(0, chunk_cols(0))
+        h_pass(LAST, CHUNKS - 1)
+        g_first = held([P, CHUNK], F32, "g_first")
+        gelu(g_first[:], acc, 0)
+        scatter(g_first, 0, 0, CHUNK)
+
+        quantize_h(1)
+        acc = y_sum(0, chunk_cols(1))
+        g_second = held([P, CHUNK], F32, "g_second")
+        gelu(g_second[:], acc, 0)
+        scatter(g_second, 0, CHUNK, 2 * CHUNK)
+
+        late_acc = []
+        for c in range(2, CHUNKS):
+            quantize_h(c)
+            late_acc.append(y_sum(0, chunk_cols(c)))
+        cast_up(nc.scalar.copy, 1, 2, reuse="h_bf1")
+        cast_up(nc.scalar.copy, 2, 3, reuse="h_bf2")
+        quantize_up(1, 2)
+        g_pair = held([P, 2 * CHUNK], F32, "g_pair", reuse="tab_words0")
+        for i, acc in enumerate(late_acc):
+            gelu(g_pair[:, chunk_cols(i)], acc, 0)
+        quantize_up(2, 3)
+        scatter(g_pair, 0, 2 * CHUNK, S)
         store(0)
 
-        def whole_tile(n, tag=None):
-            acc = psum.tile([P, S], F32, name="acc", tag="y")
-            w4_passes(acc[:], n, slice(0, S))
-            up_pass(acc[:], n, slice(0, S))
-            scatter(gelu(acc[:], n, S, tag), n, 0, S)
+
+        def whole_tile(n, g):
+            gelu(g[:], y_sum(n, slice(0, S)), n)
+            scatter(g, n, 0, S)
             store(n)
 
-        cast_up(nc.scalar.copy, 1, 2, "h_bf1")
-        cast_up(nc.scalar.copy, 2, 3, "h_bf2")
-        quantize_up(1, 2)
-        quantize_up(2, 3)
-        whole_tile(1, "g_tile1")
-        cast_up(nc.scalar.copy, 3, 5, "g_chunk3")
+        whole_tile(1, held([P, S], F32, "g_tile1"))
+        cast_up(nc.scalar.copy, 3, 5, reuse="tab_words0")
         quantize_up(3, 5)
-        whole_tile(2)
-        whole_tile(3)
-        cast_up(nc.scalar.copy, 5, 7, "g_tile1")
+        for n in range(2, 4):
+            whole_tile(n, ring.tile([P, S], F32, name="g"))
+        cast_up(nc.scalar.copy, 5, 7, reuse="g_tile1")
         cast_up(nc.scalar.copy, 7, 8)
         quantize_up(5, 7)
         quantize_up(7, 8)
         for n in range(4, TILES):
-            whole_tile(n)
+            whole_tile(n, ring.tile([P, S], F32, name="g"))

from contextlib import ExitStack

import concourse.mybir as mybir
from concourse.masks import make_identity

K, M, T, S, R = 2048, 1024, 1024, 512, 512
FLOPS = 2 * S * (K * M + K * R + R * M)

F32 = mybir.dt.float32
BF16 = mybir.dt.bfloat16
I32 = mybir.dt.int32
U32 = mybir.dt.uint32
U16 = mybir.dt.uint16
U8 = mybir.dt.uint8
FP8X4 = mybir.dt.float8_e4m3fn_x4
FP4X4 = mybir.dt.float4_e2m1fn_x4
GELU = mybir.ActivationFunctionType.Gelu_apprx_tanh
MULT = mybir.AluOpType.mult

P = 128
PACK = 4
K_PASS = P * PACK
PASSES = K // K_PASS
LAST = PASSES - 1
BLOCKS = K_PASS // 32
QUAD = 32
QUAD_ROWS = 4
ENTRIES = 16
LINE = 4
CHUNK = 128
CHUNKS = S // CHUNK
TILES = M // P
PAGES = 3
GELU_BUFS = 3
PSUM_BUFS = 4

UP_PIECES = ((0, 1), (1, 3), (3, 5), (5, 8))
W4_PIECES = ((0, 2), (2, 4), (4, 8))
W4_SCALE_PIECES = ((0, 2), (2, 8))

SHARE_WHOLE = 64
SHARE_HALF = 40


def piece_of(pieces, n):
    i = [lo <= n < hi for lo, hi in pieces].index(True)
    return i, (n - pieces[i][0]) * P


def tile_list_tabscat_l_gelu_kernel(tc, tab, w4_words, w4_scales, down, up, b, wgo, offs, offs2, out):
    nc = tc.nc
    with ExitStack() as ctx:
        keep = ctx.enter_context(tc.tile_pool(name="keep", bufs=1))
        ring = ctx.enter_context(tc.tile_pool(name="ring", bufs=GELU_BUFS))
        psum = ctx.enter_context(tc.psum_pool(name="psum", bufs=PSUM_BUFS))

        def held(shape, dtype, name, reuse=None):
            return keep.tile(shape, dtype, name=name, tag=reuse or name, align_bytes=64)

        pick = keep.tile([P, S // ENTRIES], U16, name="pick")
        place = keep.tile([P, S // ENTRIES], U16, name="place")
        tab_scales = held([P, T], U8, "tab_scales")
        dense_scales = held([P, S], U8, "dense_scales")
        got_scales = held([P, PASSES * S], U8, "got_scales")
        tab_words = {}
        got_words = [held([P, S], U32, f"got_words{a}") for a in range(LAST)]
        got_words.append(held([P, S - CHUNK], U32, f"got_words{LAST}"))
        got_tail = []
        down_bf = [held([P, R * PACK], BF16, f"down_bf{a}") for a in range(PASSES)]
        down_codes = [held([P, R], U32, f"down_codes{a}") for a in range(PASSES)]
        down_scales = [held([P, R], U8, f"down_scales{a}") for a in range(PASSES)]
        b_rows = held([P, P], F32, "b_rows")
        identity = held([P, P], F32, "identity")
        warm = held([P, 16], F32, "warm")
        pages = [held([P, T], F32, f"page{i}") for i in range(PAGES)]
        w4_scale_tiles = {}
        w4_tiles = {}
        up_raw = {}
        up_bf = {}
        up_codes = held([P, M], U32, "up_codes")
        up_scales = held([P, M], U8, "up_scales")
        h_bf = [held([P, CHUNK * PACK], BF16, f"h_bf{c}") for c in range(CHUNKS)]
        h_codes = held([P, S], U32, "h_codes")
        h_scales = held([P, S], U8, "h_scales")
        h_banks = [psum.tile([P, PACK, CHUNK], F32, name=f"h_bank{c}", tag="h") for c in range(CHUNKS)]


        def load_tab_words(a, reuse=None):
            tab_words[a] = held([P, T], I32, f"tab_words{a}", reuse)
            nc.sync.dma_start(tab_words[a][:], tab[a, 0 : K_PASS * T].bitcast(I32).rearrange("(p t) -> p t", p=P))

        def load_down(a, lo, hi, reuse=None):
            raw = held([P, PACK, hi - lo], F32, f"down_raw{a}_{lo}", reuse)
            nc.sync.dma_start(raw[:], down[a * K_PASS : (a + 1) * K_PASS, lo:hi].rearrange("(p j) r -> p j r", j=PACK))
            return raw

        def load_up(i, reuse):
            lo, hi = UP_PIECES[i]
            up_raw[i] = held([P, PACK, (hi - lo) * P], F32, f"up_raw{lo}", reuse)
            nc.sync.dma_start(up_raw[i][:], up[:, lo * P : hi * P].rearrange("(p j) n -> p j n", j=PACK))

        def load_w4(i, reuse):
            lo, hi = W4_PIECES[i]
            w4_tiles[i] = held([P, PASSES, (hi - lo) * P * 2], U8, f"w4_words{lo}", reuse)
            nc.sync.dma_start(
                w4_tiles[i][:].bitcast(I32),
                w4_words[:, :, 2 * lo * P : 2 * hi * P].bitcast(I32).rearrange("a p n -> p a n"),
            )

        def clear_w4_scales(i, engine, reuse=None):
            lo, hi = W4_SCALE_PIECES[i]
            w4_scale_tiles[i] = held([P, PASSES, (hi - lo) * P], U8, f"w4_scales{lo}", reuse)
            engine.memset(w4_scale_tiles[i][:].rearrange("p a n -> p (a n)").bitcast(I32), 0)

        def load_w4_scales(i, queue):
            lo, hi = W4_SCALE_PIECES[i]
            for r in range(QUAD_ROWS):
                queue.dma_start(
                    w4_scale_tiles[i][r:P:QUAD, :, :].bitcast(I32),
                    w4_scales[:, r:BLOCKS:QUAD_ROWS, lo * P : hi * P].bitcast(I32).rearrange("a q n -> q a n"),
                )


        def gather(dst, window, lo, hi):
            nc.vector.tensor_copy(dst, window.indirect(pick[:, lo // ENTRIES : hi // ENTRIES]))

        def gather_words(a, lo, hi):
            gather(got_words[a][:, lo:hi], tab_words[a][:].bitcast(U32), lo, hi)

        def cast_down(a, raw, m_lo, m_hi, share):
            src = raw[:].rearrange("p j (m t) -> p m j t", t=PACK)
            dst = down_bf[a][:].rearrange("p (t m j) -> p m j t", t=PACK, j=PACK)
            nc.vector.tensor_copy(dst[:, m_lo : m_lo + share], src[:, 0:share])
            nc.scalar.copy(dst[:, m_lo + share : m_hi], src[:, share : m_hi - m_lo])

        def cast_up(copy, lo, hi, reuse=None):
            i, first = piece_of(UP_PIECES, lo)
            up_bf[lo] = held([P, (hi - lo) * P * PACK], BF16, f"up_bf{lo}", reuse)
            copy(
                up_bf[lo][:].rearrange("p (c i j) -> p c j i", i=LINE, j=PACK),
                up_raw[i][:, :, first : first + (hi - lo) * P].rearrange("p j (c i) -> p c j i", i=LINE),
            )

        def quantize(codes, scales, values):
            nc.vector.quantize_mx(out=codes.bitcast(FP8X4), scales=scales, in_=values)

        def quantize_down(a):
            quantize(down_codes[a][:], down_scales[a][:], down_bf[a][:])

        def quantize_up(lo, hi):
            quantize(up_codes[:, lo * P : hi * P], up_scales[:, lo * P : hi * P], up_bf[lo][:])

        def quantize_h(c):
            cols = chunk_cols(c)
            nc.scalar.copy(h_bf[c][:].rearrange("p (n t) -> p n t", t=PACK), h_banks[c][:].rearrange("p t n -> p n t"))
            quantize(h_codes[:, cols], h_scales[:, cols], h_bf[c][:])

        def gelu(g, acc, n):
            nc.scalar.activation(g, acc[:], GELU, bias=bias[:, n : n + 1])

        def scatter(g, n, lo, hi):
            window = pages[n % PAGES][:].indirect(place[:, lo // ENTRIES : hi // ENTRIES])
            nc.vector.tensor_tensor(window, g[:], weight[:, lo:hi], MULT)

        def store(n):
            nc.sync.dma_start(out[n * P : (n + 1) * P, :], pages[n % PAGES][:])


        def chunk_cols(c):
            return slice(c * CHUNK, (c + 1) * CHUNK)

        def words_of(a, cols):
            if a == LAST and cols.start == S - CHUNK:
                return got_tail[0][:]
            return got_words[a][:, cols]

        def h_pass(a, c):
            cols = chunk_cols(c)
            for t in range(PACK):
                nc.tensor.matmul_mx(
                    out=h_banks[c][:, t, :],
                    lhsT=down_codes[a][:, t * P : (t + 1) * P].bitcast(FP8X4),
                    lhsT_scale=down_scales[a][:, t * P : (t + 1) * P],
                    rhs=words_of(a, cols).bitcast(FP8X4),
                    rhs_scale=got_scales[:, a * S + cols.start : a * S + cols.stop],
                    start=(a == 0 and t == 0),
                    stop=(a == LAST and t == PACK - 1),
                )

        def y_sum(n, cols):
            acc = psum.tile([P, cols.stop - cols.start], F32, name="acc", tag="y")
            wi, w_first = piece_of(W4_PIECES, n)
            si, s_first = piece_of(W4_SCALE_PIECES, n)
            for a in range(PASSES):
                width = CHUNK if a == LAST else cols.stop - cols.start
                for lo in range(cols.start, cols.stop, width):
                    nc.tensor.matmul_mx(
                        out=acc[:, lo - cols.start : lo - cols.start + width],
                        lhsT=w4_tiles[wi][:, a, 2 * w_first : 2 * (w_first + P)].bitcast(FP4X4),
                        lhsT_scale=w4_scale_tiles[si][:, a, s_first : s_first + P],
                        rhs=words_of(a, slice(lo, lo + width)).bitcast(FP8X4),
                        rhs_scale=got_scales[:, a * S + lo : a * S + lo + width],
                        start=(a == 0),
                        stop=False,
                    )
            nc.tensor.matmul_mx(
                out=acc[:],
                lhsT=up_codes[:, n * P : (n + 1) * P].bitcast(FP8X4),
                lhsT_scale=up_scales[:, n * P : (n + 1) * P],
                rhs=h_codes[:, cols].bitcast(FP8X4),
                rhs_scale=h_scales[:, cols],
                start=False,
                stop=True,
            )
            return acc


        nc.vector.memset(b_rows[:], 0.0)
        clear_w4_scales(0, nc.vector)
        nc.vector.memset(tab_scales[PASSES * BLOCKS : P, :].bitcast(I32), 0)
        nc.vector.memset(warm[:, 0:8], 0.0)
        nc.scalar.activation(warm[:, 8:16], warm[:, 0:8], GELU)
        nc.vector.memset(got_scales[:].bitcast(I32), 0)

        nc.sync.dma_start(pick[:], offs)
        nc.sync.dma_start(
            tab_scales[0 : PASSES * BLOCKS, :].bitcast(I32),
            tab[:, K_PASS * T :].bitcast(I32).rearrange("a (q t) -> q a t", q=BLOCKS),
        )
        load_tab_words(0)
        down_raw = [load_down(0, 0, R)]
        load_tab_words(1)
        down_raw.append(load_down(1, 0, R))
        nc.sync.dma_start(place[:], offs2)
        nc.gpsimd.dma_start(b_rows[0:TILES, :], b.rearrange("(c p) -> c p", p=P))
        load_w4_scales(0, nc.gpsimd)
        make_identity(nc, identity[:])
        for page in pages:
            nc.gpsimd.memset(page[:], 0.0)


        gather(dense_scales[:], tab_scales[:], 0, S)
        dense_rows = QUAD_ROWS * PASSES
        for q in range(P // QUAD):
            nc.sync.dma_start(
                got_scales[QUAD * q : QUAD * q + QUAD_ROWS, :].bitcast(I32).rearrange("r (a s) -> r a s", a=PASSES),
                dense_scales[dense_rows * q : dense_rows * (q + 1), :].bitcast(I32),
            )
        down_raw.append(load_down(2, 0, R, reuse="tab_scales"))

        b_turned = psum.tile([P, P], F32, name="b_turned", tag="y")
        nc.tensor.transpose(b_turned[:], b_rows[:], identity[:])
        bias = held([P, TILES], F32, "bias", reuse="dense_scales")
        nc.scalar.copy(bias[:], b_turned[:, 0:TILES])


        gather_words(0, 0, S)
        load_tab_words(2, reuse="tab_words0")
        cast_down(0, down_raw[0], 0, P, SHARE_WHOLE)
        first_half = load_down(LAST, 0, R // 2, reuse="down_raw0_0")
        quantize_down(0)
        for c in range(CHUNKS):
            h_pass(0, c)
        second_half = load_down(LAST, R // 2, R, reuse="down_bf0")

        gather_words(1, 0, S)
        load_tab_words(LAST, reuse="tab_words1")
        cast_down(1, down_raw[1], 0, P, SHARE_WHOLE)
        load_up(0, reuse="down_raw1_0")
        quantize_down(1)
        for c in range(CHUNKS):
            h_pass(1, c)
        load_w4(0, reuse="down_bf1")

        cast_down(2, down_raw[2], 0, P, SHARE_WHOLE)
        weight = held([P, S], F32, "weight", reuse="tab_scales")
        nc.sync.dma_start(weight[:], wgo)
        quantize_down(2)
        for half in range(2):
            gather_words(2, half * S // 2, (half + 1) * S // 2)
            for c in range(half * CHUNKS // 2, (half + 1) * CHUNKS // 2):
                h_pass(2, c)
        load_up(1, reuse="tab_words0")

        cast_down(LAST, first_half, 0, P // 2, SHARE_HALF)
        load_w4(1, reuse="down_raw0_0")
        cast_down(LAST, second_half, P // 2, P, SHARE_HALF)
        load_up(2, reuse="down_bf0")
        quantize_down(LAST)
        clear_w4_scales(1, nc.gpsimd, reuse=f"down_bf{LAST}")
        load_w4_scales(1, nc.sync)
        gather_words(LAST, 0, CHUNK)
        h_pass(LAST, 0)
        gather_words(LAST, CHUNK, S - CHUNK)
        for c in range(1, CHUNKS - 1):
            h_pass(LAST, c)
        cast_up(nc.vector.tensor_copy, 0, 1)
        load_w4(2, reuse="down_raw1_0")


        quantize_h(0)
        quantize_up(0, 1)
        got_tail.append(held([P, CHUNK], U32, "got_tail", reuse="h_bf0"))
        gather(got_tail[0][:], tab_words[LAST][:].bitcast(U32), S - CHUNK, S)
        load_up(3, reuse="tab_words1")
        acc = y_sum(0, chunk_cols(0))
        h_pass(LAST, CHUNKS - 1)
        g_first = held([P, CHUNK], F32, "g_first")
        gelu(g_first[:], acc, 0)
        scatter(g_first, 0, 0, CHUNK)

        quantize_h(1)
        acc = y_sum(0, chunk_cols(1))
        g_second = held([P, CHUNK], F32, "g_second")
        gelu(g_second[:], acc, 0)
        scatter(g_second, 0, CHUNK, 2 * CHUNK)

        late_acc = []
        for c in range(2, CHUNKS):
            quantize_h(c)
            late_acc.append(y_sum(0, chunk_cols(c)))
        cast_up(nc.scalar.copy, 1, 2, reuse="h_bf1")
        cast_up(nc.scalar.copy, 2, 3, reuse="h_bf2")
        quantize_up(1, 2)
        g_pair = held([P, 2 * CHUNK], F32, "g_pair", reuse="tab_words0")
        for i, acc in enumerate(late_acc):
            gelu(g_pair[:, chunk_cols(i)], acc, 0)
        quantize_up(2, 3)
        scatter(g_pair, 0, 2 * CHUNK, S)
        store(0)


        def whole_tile(n, g):
            gelu(g[:], y_sum(n, slice(0, S)), n)
            scatter(g, n, 0, S)
            store(n)

        whole_tile(1, held([P, S], F32, "g_tile1"))
        cast_up(nc.scalar.copy, 3, 5, reuse="tab_words0")
        quantize_up(3, 5)
        for n in range(2, 4):
            whole_tile(n, ring.tile([P, S], F32, name="g"))
        cast_up(nc.scalar.copy, 5, 7, reuse="g_tile1")
        cast_up(nc.scalar.copy, 7, 8)
        quantize_up(5, 7)
        quantize_up(7, 8)
        for n in range(4, TILES):
            whole_tile(n, ring.tile([P, S], F32, name="g"))
